import numpy as np, ml_dtypes
CORES = [2,3,42,43,82,83,122,123]
N = 8
import mx_ref
NC, KT, WT = 256, 4, 1
BF = ml_dtypes.bfloat16
def cut(t, i, w=512):
    return t[:, w * i:w * i + w]
def pk(c, s, i=0):
    return (np.ascontiguousarray(c[:, 512 * i:512 * i + 512]), mx_ref.live(s[:, 128 * i:128 * i + 128]))
def inputs(rng, e, E):
    def f(*shape):
        v = (rng.standard_normal(shape, dtype=np.float32) * np.exp2(rng.integers(-2, 3, shape[:-1] + (1,)))).astype(BF)
        return mx_ref.spread((v.astype(np.float32) * np.exp2(rng.integers(-E, E + 1, shape[:-2] + (1, 1))).astype(np.float32)).astype(BF), rng, e)
    def packed(k):
        c = np.zeros((N, 128, k * 512), np.uint8); s = np.zeros((N, 128, k * 128), np.uint8)
        for r in range(N):
            for i in range(k):
                a, b = mx_ref.quantize(f(128, 512)); c[r][:, 512 * i:512 * i + 512] = a; s[r][:, 128 * i:128 * i + 128] = mx_ref.plane(b, rng)
        return c, s
    d = {}
    d["wc"], d["ws"] = packed(KT * WT)
    d["x"] = f(N, 128, KT * 4 * NC)
    return d
def setup_inputs(rng):
    return inputs(rng, 0, 0)
def setup_inputs_blocks(rng):
    return inputs(rng, 2, 0)
def setup_inputs_wide(rng):
    d = inputs(rng, 0, 1); d["x"] = inputs(rng, 0, 0)["x"]
    return d
def reference(wc, ws, x):
    X = [[mx_ref.quantize(cut(x[j], t, 4 * NC)) for t in range(KT)] for j in range(N)]
    y = np.zeros((N, 128, N * WT * NC), np.float32)
    for r in range(N):
        for b in range(N * WT):
            j, i = divmod(b, WT)
            for t in range(KT):
                p = mx_ref.matmul(pk(wc[r], ws[r], KT * i + t), X[j][t])
                z = p if t == 0 else z + p
            y[r][:, NC * b:NC * b + NC] = z
    return {"y": y}

@@ -1,0 +1,230 @@
+from concourse.bass import DstId, RemoteDMATransfer
+from concourse.mybir import dt
+import comms_topo
+
+NCORES = 128
+HALF = 512
+WAYOF = {(k, i, h): "B" if h else "AC"[(k + i) % 2] for k in range(3) for i in range(2) for h in range(2)}
+ORDER = [(k, i, h) for k in range(3) for h in range(2) for i in range(2)]
+NQ = len(ORDER)
+FIRST = [2, 3, 0, 1]
+XP = 3
+YB = 2
+
+SCRATCH = {
+    "xs": ("sbuf", [128, 512 * XP], "bfloat16"),
+    "wq": ("sbuf", [128, 512], "float8_e4m3fn_x4"),
+    "wp": ("sbuf", [128, 512], "uint8"),
+    "yb": ("sbuf", [128, 256 * YB], "float32"),
+    "ps": ("psum", [128, 4096], "float32"),
+}
+for _p in range(4):
+    SCRATCH["pc%d" % _p] = ("sbuf", [128, HALF], "float8_e4m3fn_x4")
+    SCRATCH["pp%d" % _p] = ("sbuf", [128, HALF], "uint8")
+for _p in range(5):
+    SCRATCH["hc%d" % _p] = ("dram", [128, HALF], "float8_e4m3fn_x4")
+    SCRATCH["hp%d" % _p] = ("dram", [128, HALF], "uint8")
+for _q in range(NQ):
+    SCRATCH["dc%d" % _q] = ("dram", [128, HALF], "float8_e4m3fn_x4")
+    SCRATCH["dp%d" % _q] = ("dram", [128, HALF], "uint8")
+SEMAPHORES = (["x%d" % t for t in range(8)] + ["qd%d" % t for t in range(8)] + ["wl", "out", "st0", "st1"]
+              + ["hop%d" % k for k in range(3)] + ["so0", "so1", "sd", "pe0", "pe1"]
+              + ["in%d" % k for k in range(NQ)] + ["ld%d" % k for k in range(NQ)]
+              + ["mo0", "mo1", "mp0", "mp1"] + ["mm%d" % k for k in range(NQ)]
+              + ["yc%d" % b for b in range(YB)] + ["ys%d" % b for b in range(YB)])
+
+
+def count(mask):
+    return bin(mask).count("1")
+
+
+def layout(T, topo):
+    chips = []
+    for c in T.cores:
+        if topo.chip(c) not in chips:
+            chips.append(topo.chip(c))
+    plan = []
+    for ch in chips:
+        on = [c for c in range(NCORES) if topo.chip(c) == ch]
+        ranks = [c for c in T.cores if topo.chip(c) == ch]
+        far = [c for c in T.cores if topo.chip(c) != ch]
+        send = [c for c in on if topo.die(c) != topo.die(ranks[0]) and all(topo.may_write(c, d) for d in far)][:2]
+        near = [c for c in on if c not in ranks and topo.die(c) == topo.die(ranks[0])][:2]
+        relay = [c for c in range(NCORES) if topo.mates(topo.chip(c), ch) and topo.die(c) == topo.die(ranks[0])
+                 and all(topo.may_write(c, d) for d in ranks)][:2]
+        plan.append({"ranks": ranks, "A": send, "B": near, "C": relay})
+    return plan
+
+
+def put(g, topo, transfers, lsem):
+    ts = []
+    for to, src, dst, mask, rsem in transfers:
+        ids = []
+        for d in to:
+            rid, pid, _ = topo.addr(d)
+            ids.append(DstId(rid=rid, pnc=pid))
+        ts.append(RemoteDMATransfer(dst_ids=ids, dma_engine_mask=mask, remote_sem=rsem, srcs=[src], dsts=[dst] * len(ids)))
+    g.remote_dma_fused(ts, local_sem=lsem)
+
+
+def buf(T, a, n):
+    return T["%sc%d" % (a, n)][:].bitcast(dt.uint8), T["%sp%d" % (a, n)][:]
+
+
+def places():
+    user = ["own0", "own1", "peer0", "peer1"]
+    line = list(FIRST)
+    got = []
+    for q in range(NQ):
+        p = line.pop(0)
+        got.append((p, user[p]))
+        user[p] = "mm%d" % q
+        line.append(p)
+    return got
+
+
+def rank_program(g, core, T, topo):
+    plan = layout(T, topo)
+    for me, here in enumerate(plan):
+        peers = [plan[me ^ (k + 1)] for k in range(3)]
+        for w in "ABC":
+            if core in here[w]:
+                i = here[w].index(core)
+                jobs = []
+                for q, (k, i2, h) in enumerate(ORDER):
+                    if WAYOF[k, i2, h] == w and i2 == i:
+                        if w == "A":
+                            jobs.append((h, here["ranks"][i2], peers[k]["ranks"], q))
+                        else:
+                            jobs.append((k, peers[k]["ranks"][i2], here["ranks"], q))
+                forward(g, core, T, topo, jobs, topo.mask(core, peers[0]["ranks"][0]))
+        if core in here["ranks"]:
+            worker(g, core, T, topo, me, here, peers)
+
+
+def forward(g, core, T, topo, jobs, off):
+    S = T.sem
+    n = 0
+    for hq, src, to, q in jobs:
+        g.wait_ge(S["hop%d" % hq], 2 * count(off))
+        m = topo.mask(core, to[0])
+        for s, d in zip(buf(T, "h", hq), buf(T, "d", q)):
+            put(g, topo, [(to, s, d, m, S["in%d" % q])], S.out)
+            n += count(m)
+    g.wait_ge(S.out, n)
+
+
+def worker(g, core, T, topo, me, here, peers):
+    S = T.sem
+    i = here["ranks"].index(core)
+    peer = here["ranks"][1 - i]
+    mine, its = T.rank_of(core), T.rank_of(peer)
+    off = topo.mask(core, peers[0]["ranks"][0])
+    stay = topo.mask(core, peer) & ~off
+
+    def load(t):
+        q = g.sync if t % 2 == 0 else g.scalar
+        b = 512 * (t % XP)
+        if t >= XP:
+            q.wait_ge(S["qd%d" % (t - XP)], 1)
+        q.dma_start(out=T.xs[:, b:b + 512], in_=T.x[:, 512 * t:512 * t + 512]).then_inc(S["x%d" % t], 16)
+
+    def store(h):
+        for t in range(4 * h, 4 * h + 4):
+            for q in (g.sync, g.scalar):
+                q.wait_ge(S["qd%d" % t], 1)
+        for q, s, d in zip((g.sync, g.scalar), buf(T, "p", h), buf(T, "h", 3 + h)):
+            q.dma_start(out=d, in_=s).then_inc(S["st%d" % h], 16)
+    for t in range(8):
+        load(t)
+        if t == 5:
+            g.sync.dma_start(out=T.wq[:].bitcast(dt.uint8), in_=T.wc[:]).then_inc(S.wl, 16)
+            g.scalar.dma_start(out=T.wp[:], in_=T.ws[:]).then_inc(S.wl, 16)
+    store(0)
+    store(1)
+    for t in range(8):
+        b, c = 512 * (t % XP), 128 * (t % 4)
+        g.vector.wait_ge(S["x%d" % t], 16)
+        g.vector.quantize_mx(T["pc%d" % (t // 4)][:, c:c + 128], T["pp%d" % (t // 4)][:, c:c + 128], T.xs[:, b:b + 512]).then_inc(S["qd%d" % t], 1)
+
+    sent = {"so0": 0, "so1": 0, "sd": 0}
+
+    def out(to, h, src, hq, withpeer, sem):
+        for z in range(2):
+            ts = [(to, src[z], buf(T, "h", hq)[z], off, S["hop%d" % hq])]
+            if withpeer:
+                ts.append(([peer], src[z], buf(T, "p", 2 + h)[z], stay, S["pe%d" % h]))
+            put(g, topo, ts, S[sem])
+            sent[sem] += sum(count(t[3]) for t in ts)
+
+    for h in range(2):
+        for t in range(4 * h, 4 * h + 4):
+            g.wait_ge(S["qd%d" % t], 1)
+        ways = [(k, WAYOF[k, i, h]) for k in range(3)]
+        first = True
+        if "A" in [w for k, w in ways]:
+            out([here["A"][i]], h, buf(T, "p", h), h, True, "so%d" % h)
+            first = False
+        g.wait_ge(S["st%d" % h], 32)
+        for k, w in ways:
+            if w != "A":
+                out([peers[k][w][i]], h, buf(T, "h", 3 + h), k, first, "sd")
+                first = False
+    for s in sent:
+        if sent[s]:
+            g.wait_ge(S[s], sent[s])
+
+    got = places()
+    free = {}
+    for q in range(NQ):
+        free["mm%d" % q] = [("mm%d" % q, 2)]
+    for h in range(2):
+        free["own%d" % h] = [("mo%d" % h, 2), ("st%d" % h, 32)] + ([("so%d" % h, sent["so%d" % h])] if sent["so%d" % h] else [])
+        free["peer%d" % h] = [("mp%d" % h, 2)]
+    for q, (k, i2, h) in enumerate(ORDER):
+        p, b = got[q]
+        w = WAYOF[k, i2, h]
+        for s, v in free[b]:
+            g.sync.wait_ge(S[s], v)
+        g.sync.wait_ge(S["in%d" % q], 2 * count(topo.mask((peers[k] if w == "A" else here)[w][i2], core)))
+        for s, d in zip(buf(T, "d", q), buf(T, "p", p)):
+            g.sync.dma_start(out=d, in_=s).then_inc(S["ld%d" % q], 16)
+
+    seen = {}
+    users = {}
+    flushes = []
+
+    def products(j, h, p, done):
+        for u in range(2):
+            t, a = 2 * h + u, 256 * u
+            n = seen.get(j, 0)
+            seen[j] = n + 1
+            g.tensor.matmul_mx(T.ps[:, 512 * j:512 * j + 256], T.wq[:, 128 * t:128 * t + 128], T.wp[:, 128 * t:128 * t + 128],
+                               T["pc%d" % p][:, a:a + 256], T["pp%d" % p][:, a:a + 256], n == 0, n == 3).then_inc(S[done], 1)
+        users.setdefault(j, []).append(done)
+        if len(users[j]) == 2:
+            flushes.append((j, users[j]))
+
+    g.tensor.wait_ge(S.wl, 32)
+    for h in range(2):
+        for t in range(4 * h, 4 * h + 4):
+            g.tensor.wait_ge(S["qd%d" % t], 1)
+        products(mine, h, h, "mo%d" % h)
+    for h in range(2):
+        g.tensor.wait_ge(S["pe%d" % h], 2 * count(stay))
+        products(its, h, 2 + h, "mp%d" % h)
+    for q, (k, i2, h) in enumerate(ORDER):
+        g.tensor.wait_ge(S["ld%d" % q], 32)
+        products(T.rank_of(peers[k]["ranks"][i2]), h, got[q][0], "mm%d" % q)
+
+    for n, (j, d) in enumerate(flushes):
+        for s in d:
+            g.vector.wait_ge(S[s], 2)
+        b, m = n % YB, n // YB
+        if m:
+            g.vector.wait_ge(S["ys%d" % b], 16 * m)
+        g.vector.tensor_copy(T.yb[:, 256 * b:256 * b + 256], T.ps[:, 512 * j:512 * j + 256]).then_inc(S["yc%d" % b], 1)
+        g.scalar.wait_ge(S["yc%d" % b], m + 1)
+        g.scalar.dma_start(out=T.y[:, 256 * j:256 * j + 256], in_=T.yb[:, 256 * b:256 * b + 256]).then_inc(S["ys%d" % b], 16)
+    for b in range(YB):
+        g.vector.wait_ge(S["ys%d" % b], 16 * len(range(b, len(flushes), YB)))

@@ -4,12 +4,15 @@ import comms_topo
 
 NCORES = 128
 HALF = 512
-WAYOF = {(k, i, h): "B" if h else "AC"[(k + i) % 2] for k in range(3) for i in range(2) for h in range(2)}
-ORDER = [(k, i, h) for k in range(3) for h in range(2) for i in range(2)]
-NQ = len(ORDER)
-FIRST = [2, 3, 0, 1]
 XP = 3
 YB = 2
+RELAYED = ((0, 1), (2, 0))
+ORDER = [(k, i, h) for k in range(3) for h in (1, 0) for i in range(2)]
+NQ = len(ORDER)
+DIRECT = (0, 2, 4, 5)
+SEQ = (0, 2, 4, 5, 1, 3, 6, 7, 8, 9, 10, 11)
+FIRST = (2, 3, 0, 1)
+HOP = ("ac", "ap")
 
 SCRATCH = {
     "xs": ("sbuf", [128, 512 * XP], "bfloat16"),
@@ -21,16 +24,17 @@ SCRATCH = {
 for _p in range(4):
     SCRATCH["pc%d" % _p] = ("sbuf", [128, HALF], "float8_e4m3fn_x4")
     SCRATCH["pp%d" % _p] = ("sbuf", [128, HALF], "uint8")
-for _p in range(5):
-    SCRATCH["hc%d" % _p] = ("dram", [128, HALF], "float8_e4m3fn_x4")
-    SCRATCH["hp%d" % _p] = ("dram", [128, HALF], "uint8")
+for _k in range(3):
+    SCRATCH["hc%d" % _k] = ("dram", [128, HALF], "float8_e4m3fn_x4")
+    SCRATCH["hp%d" % _k] = ("dram", [128, HALF], "uint8")
 for _q in range(NQ):
-    SCRATCH["dc%d" % _q] = ("dram", [128, HALF], "float8_e4m3fn_x4")
-    SCRATCH["dp%d" % _q] = ("dram", [128, HALF], "uint8")
-SEMAPHORES = (["x%d" % t for t in range(8)] + ["qd%d" % t for t in range(8)] + ["wl", "out", "st0", "st1"]
-              + ["hop%d" % k for k in range(3)] + ["so0", "so1", "sd", "pe0", "pe1"]
-              + ["in%d" % k for k in range(NQ)] + ["ld%d" % k for k in range(NQ)]
-              + ["mo0", "mo1", "mp0", "mp1"] + ["mm%d" % k for k in range(NQ)]
+    if _q not in DIRECT:
+        SCRATCH["dc%d" % _q] = ("dram", [128, HALF], "float8_e4m3fn_x4")
+        SCRATCH["dp%d" % _q] = ("dram", [128, HALF], "uint8")
+SEMAPHORES = (["x%d" % t for t in range(8)] + ["qd%d" % t for t in range(8)] + ["wl", "out", "cl"]
+              + ["%s%d" % (a, k) for a in HOP for k in range(3)] + ["so0", "so1", "pe0", "pe1"]
+              + ["in%d" % q for q in range(NQ)] + ["ld%d" % q for q in range(NQ)] + ["cr%d" % q for q in range(NQ)]
+              + ["mm%d" % q for q in range(NQ)] + ["mo0", "mo1", "mp0", "mp1"]
               + ["yc%d" % b for b in range(YB)] + ["ys%d" % b for b in range(YB)])
 
 
@@ -48,11 +52,13 @@ def layout(T, topo):
         on = [c for c in range(NCORES) if topo.chip(c) == ch]
         ranks = [c for c in T.cores if topo.chip(c) == ch]
         far = [c for c in T.cores if topo.chip(c) != ch]
-        send = [c for c in on if topo.die(c) != topo.die(ranks[0]) and all(topo.may_write(c, d) for d in far)][:2]
-        near = [c for c in on if c not in ranks and topo.die(c) == topo.die(ranks[0])][:2]
-        relay = [c for c in range(NCORES) if topo.mates(topo.chip(c), ch) and topo.die(c) == topo.die(ranks[0])
-                 and all(topo.may_write(c, d) for d in ranks)][:2]
-        plan.append({"ranks": ranks, "A": send, "B": near, "C": relay})
+        d = topo.die(ranks[0])
+        send = [c for c in on if topo.die(c) != d and all(topo.may_write(c, f) for f in far)][:2]
+        land = [c for c in on if c not in ranks + send]
+        relay = [c for c in range(NCORES) if topo.mates(topo.chip(c), ch) and all(topo.may_write(c, r) for r in ranks)]
+        plan.append({"ranks": ranks, "S": send,
+                     "L": [[c for c in land if (topo.die(c) == d) == s][:2] for s in (False, True)],
+                     "R": [[c for c in relay if (topo.die(c) == d) == s][:2] for s in (False, True)]})
     return plan
 
 
@@ -71,13 +77,18 @@ def buf(T, a, n):
     return T["%sc%d" % (a, n)][:].bitcast(dt.uint8), T["%sp%d" % (a, n)][:]
 
 
+def between(dst, q):
+    k, i, h = ORDER[q]
+    return dst["R" if (k, i) in RELAYED else "L"][h][i]
+
+
 def places():
-    user = ["own0", "own1", "peer0", "peer1"]
+    user = ["mo0", "mo1", "mp0", "mp1"]
     line = list(FIRST)
-    got = []
-    for q in range(NQ):
+    got = {}
+    for q in SEQ:
         p = line.pop(0)
-        got.append((p, user[p]))
+        got[q] = (p, user[p])
         user[p] = "mm%d" % q
         line.append(p)
     return got
@@ -87,114 +98,125 @@ def rank_program(g, core, T, topo):
     plan = layout(T, topo)
     for me, here in enumerate(plan):
         peers = [plan[me ^ (k + 1)] for k in range(3)]
-        for w in "ABC":
-            if core in here[w]:
-                i = here[w].index(core)
-                jobs = []
-                for q, (k, i2, h) in enumerate(ORDER):
-                    if WAYOF[k, i2, h] == w and i2 == i:
-                        if w == "A":
-                            jobs.append((h, here["ranks"][i2], peers[k]["ranks"], q))
-                        else:
-                            jobs.append((k, peers[k]["ranks"][i2], here["ranks"], q))
-                forward(g, core, T, topo, jobs, topo.mask(core, peers[0]["ranks"][0]))
+        off = topo.mask(here["ranks"][0], peers[0]["ranks"][0])
+        if core in here["S"]:
+            sender(g, core, T, topo, here, peers, off)
+        jobs = [q for q in SEQ if between(here, q) == core]
+        if jobs:
+            forward(g, core, T, topo, here, jobs, off)
         if core in here["ranks"]:
-            worker(g, core, T, topo, me, here, peers)
+            worker(g, core, T, topo, here, peers, off)
 
 
-def forward(g, core, T, topo, jobs, off):
+def sender(g, core, T, topo, here, peers, off):
     S = T.sem
+    i = here["S"].index(core)
+    w = count(topo.mask(here["ranks"][i], core))
     n = 0
-    for hq, src, to, q in jobs:
-        g.wait_ge(S["hop%d" % hq], 2 * count(off))
-        m = topo.mask(core, to[0])
-        for s, d in zip(buf(T, "h", hq), buf(T, "d", q)):
-            put(g, topo, [(to, s, d, m, S["in%d" % q])], S.out)
+    for k in range(3):
+        to = [between(peers[k], ORDER.index((k, i, 0)))]
+        for z in range(2):
+            if k == 0:
+                g.wait_ge(S["%s0" % HOP[z]], w)
+            put(g, topo, [(to, buf(T, "h", 0)[z], buf(T, "h", k)[z], off, S["%s%d" % (HOP[z], k)])], S.out)
+            n += count(off)
+    g.wait_ge(S.out, n)
+
+
+def forward(g, core, T, topo, here, jobs, off):
+    S = T.sem
+    m = topo.mask(core, here["ranks"][0])
+    got = places()
+    n = 0
+    for q in jobs:
+        k = ORDER[q][0]
+        dst = buf(T, "p", got[q][0]) if q in DIRECT else buf(T, "d", q)
+        if q in DIRECT:
+            g.wait_ge(S["cr%d" % q], len(here["ranks"]))
+        for z in range(2):
+            g.wait_ge(S["%s%d" % (HOP[z], k)], count(off))
+            put(g, topo, [(here["ranks"], buf(T, "h", k)[z], dst[z], m, S["in%d" % q])], S.out)
             n += count(m)
     g.wait_ge(S.out, n)
 
 
-def worker(g, core, T, topo, me, here, peers):
+def worker(g, core, T, topo, here, peers, off):
     S = T.sem
     i = here["ranks"].index(core)
     peer = here["ranks"][1 - i]
     mine, its = T.rank_of(core), T.rank_of(peer)
-    off = topo.mask(core, peers[0]["ranks"][0])
+    snd = here["S"][i]
+    whole = topo.mask(core, snd)
     stay = topo.mask(core, peer) & ~off
 
-    def load(t):
+    for t in range(8):
         q = g.sync if t % 2 == 0 else g.scalar
         b = 512 * (t % XP)
         if t >= XP:
             q.wait_ge(S["qd%d" % (t - XP)], 1)
         q.dma_start(out=T.xs[:, b:b + 512], in_=T.x[:, 512 * t:512 * t + 512]).then_inc(S["x%d" % t], 16)
-
-    def store(h):
-        for t in range(4 * h, 4 * h + 4):
-            for q in (g.sync, g.scalar):
-                q.wait_ge(S["qd%d" % t], 1)
-        for q, s, d in zip((g.sync, g.scalar), buf(T, "p", h), buf(T, "h", 3 + h)):
-            q.dma_start(out=d, in_=s).then_inc(S["st%d" % h], 16)
-    for t in range(8):
-        load(t)
-        if t == 5:
-            g.sync.dma_start(out=T.wq[:].bitcast(dt.uint8), in_=T.wc[:]).then_inc(S.wl, 16)
-            g.scalar.dma_start(out=T.wp[:], in_=T.ws[:]).then_inc(S.wl, 16)
-    store(0)
-    store(1)
+    for q in (g.sync, g.scalar):
+        q.wait_ge(S.qd5, 1)
+    g.sync.dma_start(out=T.wq[:].bitcast(dt.uint8), in_=T.wc[:]).then_inc(S.wl, 16)
+    g.scalar.dma_start(out=T.wp[:], in_=T.ws[:]).then_inc(S.wl, 16)
     for t in range(8):
         b, c = 512 * (t % XP), 128 * (t % 4)
         g.vector.wait_ge(S["x%d" % t], 16)
-        g.vector.quantize_mx(T["pc%d" % (t // 4)][:, c:c + 128], T["pp%d" % (t // 4)][:, c:c + 128], T.xs[:, b:b + 512]).then_inc(S["qd%d" % t], 1)
+        g.vector.quantize_mx(T["pc%d" % (t // 4)][:, c:c + 128], T["pp%d" % (t // 4)][:, c:c + 128],
+                             T.xs[:, b:b + 512]).then_inc(S["qd%d" % t], 1)
 
-    sent = {"so0": 0, "so1": 0, "sd": 0}
-
-    def out(to, h, src, hq, withpeer, sem):
+    sent = [0, 0]
+    for t in range(4):
+        g.wait_ge(S["qd%d" % t], 1)
+    for z in range(2):
+        put(g, topo, [([snd], buf(T, "p", 0)[z], buf(T, "h", 0)[z], whole, S["%s0" % HOP[z]])], S.so0)
+        sent[0] += count(whole)
+    for t in range(4, 8):
+        g.wait_ge(S["qd%d" % t], 1)
+    for k in range(3):
+        to = [between(peers[k], ORDER.index((k, i, 1)))]
         for z in range(2):
-            ts = [(to, src[z], buf(T, "h", hq)[z], off, S["hop%d" % hq])]
-            if withpeer:
-                ts.append(([peer], src[z], buf(T, "p", 2 + h)[z], stay, S["pe%d" % h]))
-            put(g, topo, ts, S[sem])
-            sent[sem] += sum(count(t[3]) for t in ts)
-
-    for h in range(2):
-        for t in range(4 * h, 4 * h + 4):
-            g.wait_ge(S["qd%d" % t], 1)
-        ways = [(k, WAYOF[k, i, h]) for k in range(3)]
-        first = True
-        if "A" in [w for k, w in ways]:
-            out([here["A"][i]], h, buf(T, "p", h), h, True, "so%d" % h)
-            first = False
-        g.wait_ge(S["st%d" % h], 32)
-        for k, w in ways:
-            if w != "A":
-                out([peers[k][w][i]], h, buf(T, "h", 3 + h), k, first, "sd")
-                first = False
-    for s in sent:
-        if sent[s]:
-            g.wait_ge(S[s], sent[s])
+            ts = [(to, buf(T, "p", 1)[z], buf(T, "h", k)[z], off, S["%s%d" % (HOP[z], k)])]
+            if k < 2:
+                ts.append(([peer], buf(T, "p", k)[z], buf(T, "p", 2 + k)[z], stay, S["pe%d" % k]))
+            put(g, topo, ts, S.so1)
+            sent[1] += sum(count(t[3]) for t in ts)
 
     got = places()
-    free = {}
-    for q in range(NQ):
-        free["mm%d" % q] = [("mm%d" % q, 2)]
+    offers = 0
+    for q in SEQ:
+        x = between(here, q)
+        p, before = got[q]
+        line = g if q in DIRECT else g.sync
+        line.wait_ge(S[before], 2)
+        if before in ("mo0", "mo1"):
+            for h in range(2):
+                line.wait_ge(S["so%d" % h], sent[h])
+        if q in DIRECT:
+            rid, pid, _ = topo.addr(x)
+            g.remote_sem_update(S["cr%d" % q], S.cl, pid, rid, stay & -stay)
+            offers += 1
+        else:
+            g.sync.wait_ge(S["in%d" % q], 2 * count(topo.mask(x, core)))
+            for s, d in zip(buf(T, "d", q), buf(T, "p", p)):
+                g.sync.dma_start(out=d, in_=s).then_inc(S["ld%d" % q], 16)
+    g.wait_ge(S.cl, offers)
     for h in range(2):
-        free["own%d" % h] = [("mo%d" % h, 2), ("st%d" % h, 32)] + ([("so%d" % h, sent["so%d" % h])] if sent["so%d" % h] else [])
-        free["peer%d" % h] = [("mp%d" % h, 2)]
-    for q, (k, i2, h) in enumerate(ORDER):
-        p, b = got[q]
-        w = WAYOF[k, i2, h]
-        for s, v in free[b]:
-            g.sync.wait_ge(S[s], v)
-        g.sync.wait_ge(S["in%d" % q], 2 * count(topo.mask((peers[k] if w == "A" else here)[w][i2], core)))
-        for s, d in zip(buf(T, "d", q), buf(T, "p", p)):
-            g.sync.dma_start(out=d, in_=s).then_inc(S["ld%d" % q], 16)
+        g.wait_ge(S["so%d" % h], sent[h])
 
+    items = [(mine, h, h, [("qd%d" % t, 1) for t in range(4 * h, 4 * h + 4)], "mo%d" % h) for h in range(2)]
+    items += [(its, h, 2 + h, [("pe%d" % h, 2 * count(stay))], "mp%d" % h) for h in range(2)]
+    for q in SEQ:
+        k, i2, h = ORDER[q]
+        w = ("in%d" % q, 2 * count(topo.mask(between(here, q), core))) if q in DIRECT else ("ld%d" % q, 32)
+        items.append((T.rank_of(peers[k]["ranks"][i2]), h, got[q][0], [w], "mm%d" % q))
     seen = {}
     users = {}
     flushes = []
-
-    def products(j, h, p, done):
+    g.tensor.wait_ge(S.wl, 32)
+    for j, h, p, waits, done in items:
+        for s, v in waits:
+            g.tensor.wait_ge(S[s], v)
         for u in range(2):
             t, a = 2 * h + u, 256 * u
             n = seen.get(j, 0)
@@ -202,20 +224,8 @@ def worker(g, core, T, topo, me, here, peers):
             g.tensor.matmul_mx(T.ps[:, 512 * j:512 * j + 256], T.wq[:, 128 * t:128 * t + 128], T.wp[:, 128 * t:128 * t + 128],
                                T["pc%d" % p][:, a:a + 256], T["pp%d" % p][:, a:a + 256], n == 0, n == 3).then_inc(S[done], 1)
         users.setdefault(j, []).append(done)
-        if len(users[j]) == 2:
+        if seen[j] == 4:
             flushes.append((j, users[j]))
-
-    g.tensor.wait_ge(S.wl, 32)
-    for h in range(2):
-        for t in range(4 * h, 4 * h + 4):
-            g.tensor.wait_ge(S["qd%d" % t], 1)
-        products(mine, h, h, "mo%d" % h)
-    for h in range(2):
-        g.tensor.wait_ge(S["pe%d" % h], 2 * count(stay))
-        products(its, h, 2 + h, "mp%d" % h)
-    for q, (k, i2, h) in enumerate(ORDER):
-        g.tensor.wait_ge(S["ld%d" % q], 32)
-        products(T.rank_of(peers[k]["ranks"][i2]), h, got[q][0], "mm%d" % q)
 
     for n, (j, d) in enumerate(flushes):
         for s in d:

from concourse.bass import DstId, RemoteDMATransfer
from concourse.mybir import dt
import comms_topo

NCORES = 128
HALF = 512
XP = 3
YB = 2
RELAYED = ((0, 1), (2, 0))
ORDER = [(k, i, h) for k in range(3) for h in (1, 0) for i in range(2)]
NQ = len(ORDER)
DIRECT = (0, 2, 4, 5)
SEQ = (0, 2, 4, 5, 1, 3, 6, 7, 8, 9, 10, 11)
FIRST = (2, 3, 0, 1)
HOP = ("ac", "ap")

SCRATCH = {
    "xs": ("sbuf", [128, 512 * XP], "bfloat16"),
    "wq": ("sbuf", [128, 512], "float8_e4m3fn_x4"),
    "wp": ("sbuf", [128, 512], "uint8"),
    "yb": ("sbuf", [128, 256 * YB], "float32"),
    "ps": ("psum", [128, 4096], "float32"),
}
for _p in range(4):
    SCRATCH["pc%d" % _p] = ("sbuf", [128, HALF], "float8_e4m3fn_x4")
    SCRATCH["pp%d" % _p] = ("sbuf", [128, HALF], "uint8")
for _k in range(3):
    SCRATCH["hc%d" % _k] = ("dram", [128, HALF], "float8_e4m3fn_x4")
    SCRATCH["hp%d" % _k] = ("dram", [128, HALF], "uint8")
for _q in range(NQ):
    if _q not in DIRECT:
        SCRATCH["dc%d" % _q] = ("dram", [128, HALF], "float8_e4m3fn_x4")
        SCRATCH["dp%d" % _q] = ("dram", [128, HALF], "uint8")
SEMAPHORES = (["x%d" % t for t in range(8)] + ["qd%d" % t for t in range(8)] + ["wl", "out", "cl"]
              + ["%s%d" % (a, k) for a in HOP for k in range(3)] + ["so0", "so1", "pe0", "pe1"]
              + ["in%d" % q for q in range(NQ)] + ["ld%d" % q for q in range(NQ)] + ["cr%d" % q for q in range(NQ)]
              + ["mm%d" % q for q in range(NQ)] + ["mo0", "mo1", "mp0", "mp1"]
              + ["yc%d" % b for b in range(YB)] + ["ys%d" % b for b in range(YB)])


def count(mask):
    return bin(mask).count("1")


def layout(T, topo):
    chips = []
    for c in T.cores:
        if topo.chip(c) not in chips:
            chips.append(topo.chip(c))
    plan = []
    for ch in chips:
        on = [c for c in range(NCORES) if topo.chip(c) == ch]
        ranks = [c for c in T.cores if topo.chip(c) == ch]
        far = [c for c in T.cores if topo.chip(c) != ch]
        d = topo.die(ranks[0])
        send = [c for c in on if topo.die(c) != d and all(topo.may_write(c, f) for f in far)][:2]
        land = [c for c in on if c not in ranks + send]
        relay = [c for c in range(NCORES) if topo.mates(topo.chip(c), ch) and all(topo.may_write(c, r) for r in ranks)]
        plan.append({"ranks": ranks, "S": send,
                     "L": [[c for c in land if (topo.die(c) == d) == s][:2] for s in (False, True)],
                     "R": [[c for c in relay if (topo.die(c) == d) == s][:2] for s in (False, True)]})
    return plan


def put(g, topo, transfers, lsem):
    ts = []
    for to, src, dst, mask, rsem in transfers:
        ids = []
        for d in to:
            rid, pid, _ = topo.addr(d)
            ids.append(DstId(rid=rid, pnc=pid))
        ts.append(RemoteDMATransfer(dst_ids=ids, dma_engine_mask=mask, remote_sem=rsem, srcs=[src], dsts=[dst] * len(ids)))
    g.remote_dma_fused(ts, local_sem=lsem)


def buf(T, a, n):
    return T["%sc%d" % (a, n)][:].bitcast(dt.uint8), T["%sp%d" % (a, n)][:]


def between(dst, q):
    k, i, h = ORDER[q]
    return dst["R" if (k, i) in RELAYED else "L"][h][i]


def places():
    user = ["mo0", "mo1", "mp0", "mp1"]
    line = list(FIRST)
    got = {}
    for q in SEQ:
        p = line.pop(0)
        got[q] = (p, user[p])
        user[p] = "mm%d" % q
        line.append(p)
    return got


def rank_program(g, core, T, topo):
    plan = layout(T, topo)
    for me, here in enumerate(plan):
        peers = [plan[me ^ (k + 1)] for k in range(3)]
        off = topo.mask(here["ranks"][0], peers[0]["ranks"][0])
        if core in here["S"]:
            sender(g, core, T, topo, here, peers, off)
        jobs = [q for q in SEQ if between(here, q) == core]
        if jobs:
            forward(g, core, T, topo, here, jobs, off)
        if core in here["ranks"]:
            worker(g, core, T, topo, here, peers, off)


def sender(g, core, T, topo, here, peers, off):
    S = T.sem
    i = here["S"].index(core)
    w = count(topo.mask(here["ranks"][i], core))
    n = 0
    for k in range(3):
        to = [between(peers[k], ORDER.index((k, i, 0)))]
        for z in range(2):
            if k == 0:
                g.wait_ge(S["%s0" % HOP[z]], w)
            put(g, topo, [(to, buf(T, "h", 0)[z], buf(T, "h", k)[z], off, S["%s%d" % (HOP[z], k)])], S.out)
            n += count(off)
    g.wait_ge(S.out, n)


def forward(g, core, T, topo, here, jobs, off):
    S = T.sem
    m = topo.mask(core, here["ranks"][0])
    got = places()
    n = 0
    for q in jobs:
        k = ORDER[q][0]
        dst = buf(T, "p", got[q][0]) if q in DIRECT else buf(T, "d", q)
        if q in DIRECT:
            g.wait_ge(S["cr%d" % q], len(here["ranks"]))
        for z in range(2):
            g.wait_ge(S["%s%d" % (HOP[z], k)], count(off))
            put(g, topo, [(here["ranks"], buf(T, "h", k)[z], dst[z], m, S["in%d" % q])], S.out)
            n += count(m)
    g.wait_ge(S.out, n)


def worker(g, core, T, topo, here, peers, off):
    S = T.sem
    i = here["ranks"].index(core)
    peer = here["ranks"][1 - i]
    mine, its = T.rank_of(core), T.rank_of(peer)
    snd = here["S"][i]
    whole = topo.mask(core, snd)
    stay = topo.mask(core, peer) & ~off

    for t in range(8):
        q = g.sync if t % 2 == 0 else g.scalar
        b = 512 * (t % XP)
        if t >= XP:
            q.wait_ge(S["qd%d" % (t - XP)], 1)
        q.dma_start(out=T.xs[:, b:b + 512], in_=T.x[:, 512 * t:512 * t + 512]).then_inc(S["x%d" % t], 16)
    for q in (g.sync, g.scalar):
        q.wait_ge(S.qd5, 1)
    g.sync.dma_start(out=T.wq[:].bitcast(dt.uint8), in_=T.wc[:]).then_inc(S.wl, 16)
    g.scalar.dma_start(out=T.wp[:], in_=T.ws[:]).then_inc(S.wl, 16)
    for t in range(8):
        b, c = 512 * (t % XP), 128 * (t % 4)
        g.vector.wait_ge(S["x%d" % t], 16)
        g.vector.quantize_mx(T["pc%d" % (t // 4)][:, c:c + 128], T["pp%d" % (t // 4)][:, c:c + 128],
                             T.xs[:, b:b + 512]).then_inc(S["qd%d" % t], 1)

    sent = [0, 0]
    for t in range(4):
        g.wait_ge(S["qd%d" % t], 1)
    for z in range(2):
        put(g, topo, [([snd], buf(T, "p", 0)[z], buf(T, "h", 0)[z], whole, S["%s0" % HOP[z]])], S.so0)
        sent[0] += count(whole)
    for t in range(4, 8):
        g.wait_ge(S["qd%d" % t], 1)
    for k in range(3):
        to = [between(peers[k], ORDER.index((k, i, 1)))]
        for z in range(2):
            ts = [(to, buf(T, "p", 1)[z], buf(T, "h", k)[z], off, S["%s%d" % (HOP[z], k)])]
            if k < 2:
                ts.append(([peer], buf(T, "p", k)[z], buf(T, "p", 2 + k)[z], stay, S["pe%d" % k]))
            put(g, topo, ts, S.so1)
            sent[1] += sum(count(t[3]) for t in ts)

    got = places()
    offers = 0
    for q in SEQ:
        x = between(here, q)
        p, before = got[q]
        line = g if q in DIRECT else g.sync
        line.wait_ge(S[before], 2)
        if before in ("mo0", "mo1"):
            for h in range(2):
                line.wait_ge(S["so%d" % h], sent[h])
        if q in DIRECT:
            rid, pid, _ = topo.addr(x)
            g.remote_sem_update(S["cr%d" % q], S.cl, pid, rid, stay & -stay)
            offers += 1
        else:
            g.sync.wait_ge(S["in%d" % q], 2 * count(topo.mask(x, core)))
            for s, d in zip(buf(T, "d", q), buf(T, "p", p)):
                g.sync.dma_start(out=d, in_=s).then_inc(S["ld%d" % q], 16)
    g.wait_ge(S.cl, offers)
    for h in range(2):
        g.wait_ge(S["so%d" % h], sent[h])

    items = [(mine, h, h, [("qd%d" % t, 1) for t in range(4 * h, 4 * h + 4)], "mo%d" % h) for h in range(2)]
    items += [(its, h, 2 + h, [("pe%d" % h, 2 * count(stay))], "mp%d" % h) for h in range(2)]
    for q in SEQ:
        k, i2, h = ORDER[q]
        w = ("in%d" % q, 2 * count(topo.mask(between(here, q), core))) if q in DIRECT else ("ld%d" % q, 32)
        items.append((T.rank_of(peers[k]["ranks"][i2]), h, got[q][0], [w], "mm%d" % q))
    seen = {}
    users = {}
    flushes = []
    g.tensor.wait_ge(S.wl, 32)
    for j, h, p, waits, done in items:
        for s, v in waits:
            g.tensor.wait_ge(S[s], v)
        for u in range(2):
            t, a = 2 * h + u, 256 * u
            n = seen.get(j, 0)
            seen[j] = n + 1
            g.tensor.matmul_mx(T.ps[:, 512 * j:512 * j + 256], T.wq[:, 128 * t:128 * t + 128], T.wp[:, 128 * t:128 * t + 128],
                               T["pc%d" % p][:, a:a + 256], T["pp%d" % p][:, a:a + 256], n == 0, n == 3).then_inc(S[done], 1)
        users.setdefault(j, []).append(done)
        if seen[j] == 4:
            flushes.append((j, users[j]))

    for n, (j, d) in enumerate(flushes):
        for s in d:
            g.vector.wait_ge(S[s], 2)
        b, m = n % YB, n // YB
        if m:
            g.vector.wait_ge(S["ys%d" % b], 16 * m)
        g.vector.tensor_copy(T.yb[:, 256 * b:256 * b + 256], T.ps[:, 512 * j:512 * j + 256]).then_inc(S["yc%d" % b], 1)
        g.scalar.wait_ge(S["yc%d" % b], m + 1)
        g.scalar.dma_start(out=T.y[:, 256 * j:256 * j + 256], in_=T.yb[:, 256 * b:256 * b + 256]).then_inc(S["ys%d" % b], 16)
    for b in range(YB):
        g.vector.wait_ge(S["ys%d" % b], 16 * len(range(b, len(flushes), YB)))
